import numpy as np
import ml_dtypes


def mxq(x, axis, fmt="e4m3"):
    dtype, down = {"e4m3": (ml_dtypes.float8_e4m3fn, 7), "e5m2": (ml_dtypes.float8_e5m2, 14)}[fmt]
    v = np.moveaxis(np.asarray(x, np.float32).astype(ml_dtypes.bfloat16).astype(np.float64), axis, -1)
    blocks = v.reshape(v.shape[:-1] + (-1, 32))
    amax = np.abs(blocks).max(-1, keepdims=True)
    byte = np.maximum(np.where(amax > 0, np.frexp(amax)[1] - 1 + 127, 0) - down, 1)
    scale = np.exp2(byte - 127.0)
    codes = (blocks / scale).astype(np.float32).astype(dtype).astype(np.float64)
    return np.moveaxis((codes * scale).reshape(v.shape), -1, axis)


WIDE = False


def mx_kscale(k):
    if not WIDE:
        return np.ones(k)
    levels = np.array([10, -10, 5, -5, 0])
    if k % 512:
        return np.exp2(np.random.permutation(np.resize(levels, k // 32))).repeat(32)
    a = np.empty((k // 512, 16))
    for p in range(k // 512):
        a[p, :8] = np.random.permutation(np.resize(levels, 8))
        for g in range(8):
            far = levels[np.abs(levels - a[p, g]) >= 10]
            a[p, g + 8] = far[np.random.randint(len(far))]
    return np.exp2(a.ravel()).repeat(32)


def f64(x):
    return np.asarray(x).astype(np.float64)


def striped(idx):
    return np.tile(idx.reshape(-1, 16).T, (8, 1)).astype(np.uint16)


def unstriped(offs):
    return offs[:16].T.reshape(-1).astype(np.int64)


def striped8(idx):
    return np.concatenate([x.reshape(-1, 16).T for x in idx]).astype(np.uint16)


def runs(offs, k):
    lists = np.stack([offs[16 * r : 16 * r + 16].T.reshape(-1) for r in range(8)]).astype(np.int64)
    return lists[np.arange(k) % 512 // 64]


def pack_weight(w):
    k, n = w.shape
    w = f64(np.asarray(w, np.float32).astype(ml_dtypes.bfloat16)).reshape(k // 32, 32, n)
    amax = np.abs(w).max(1)
    byte = np.clip(np.where(amax > 0, np.frexp(amax)[1] - 1 + 127 - 7, 1), 1, 254)
    scaled = (w * np.exp2(127.0 - byte)[:, None, :]).reshape(k, n).astype(np.float32)
    words = np.ascontiguousarray(scaled.reshape(k // 512, 128, 4, n).transpose(0, 1, 3, 2)).astype(ml_dtypes.float8_e4m3fn).view(np.uint8)
    return words, np.ascontiguousarray(byte.astype(np.uint8).reshape(k // 512, 16, n))


def unpack_weight(words, scales):
    g, p, n, _ = words.shape
    vals = np.ascontiguousarray(words).view(ml_dtypes.float8_e4m3fn).astype(np.float64) * np.repeat(np.exp2(scales.astype(np.float64) - 127.0), 8, axis=1)[..., None]
    return vals.transpose(0, 1, 3, 2).reshape(g * 512, n)


def relu(v):
    return np.maximum(v, 0.0)


K, T, S, N, G, H, W = 512, 1024, 512, 512, 2048, 512, 384


def setup_inputs():
    n = np.random.standard_normal
    s = mx_kscale(K)[:, None]
    u = mx_kscale(S)
    packed_xT = pack_weight(n((K, T)) * s)
    packed_dT = pack_weight(n((K, G)) / s)
    return {
        "x_words": packed_xT[0],
        "x_scales": packed_xT[1],
        "d_words": packed_dT[0],
        "d_scales": packed_dT[1],
        "gn": (np.random.uniform(0.5, 1.5, (H, 1)) * u[:, None]).astype(np.float32),
        "w1": (n((H, N)) / np.sqrt(2 * H) / u[:, None]).astype(np.float32),
        "w2": (n((K, N)) / np.sqrt(2 * K) / s).astype(np.float32),
        "offs": striped(np.random.permutation(T)[:S]),
        "k1": striped8(np.random.randint(0, G, (8, H))),
        "n1": striped8(np.stack([np.random.permutation(S) for _ in range(8)])),
        "n2": striped8(np.stack([np.random.permutation(S) for _ in range(8)])),
        "two": striped(np.random.permutation(T)[:S]),
        "n3": striped(np.random.permutation(S)[:W]),
        "n4": striped(np.random.permutation(S)[:W]),
    }


def reference(x_words, x_scales, d_words, d_scales, gn, w1, w2, offs, k1, n1, n2, two, n3, n4):
    d_k1 = unpack_weight(d_words, d_scales)[np.arange(K)[:, None], runs(k1, K)]
    xq = unpack_weight(x_words, x_scales)[:, unstriped(offs)]
    h = 0.0625 * (d_k1.T @ xq)
    pa = h - (h[np.arange(H)[:, None], runs(n1, H)])
    pb = h[np.arange(H)[:, None], runs(n2, H)] - h
    z = f64(gn) * (relu(np.minimum(pa, pb)) - (relu(-1.0 * np.maximum(pa, pb))))
    x_two = unpack_weight(x_words, x_scales)[:, unstriped(two)]
    h2 = mxq(f64(w1), 0, "e4m3").T @ mxq(z, 0, "e4m3") + mxq(f64(w2), 0, "e4m3").T @ x_two
    old = h2[:, unstriped(n3)]
    pa2 = h2[:, unstriped(n4)]
    ra = old - (0.5 * pa2)
    out = h2.copy()
    out[:, unstriped(n3)] = ra
    return out

@@ -1,0 +1,249 @@
+from contextlib import ExitStack
+
+import concourse.mybir as mybir
+from concourse.masks import make_identity
+
+K, T, S, N, G, H, W = 512, 1024, 512, 512, 2048, 512, 384
+FLOPS = 3 * 2 * 512 * 512 * 512
+
+F32 = mybir.dt.float32
+BF16 = mybir.dt.bfloat16
+U32 = mybir.dt.uint32
+I32 = mybir.dt.int32
+U16 = mybir.dt.uint16
+U8 = mybir.dt.uint8
+FP8X4 = mybir.dt.float8_e4m3fn_x4
+ALU = mybir.AluOpType
+COPY = mybir.ActivationFunctionType.Copy
+
+P = 128
+PACK = 4
+HALF = S // 2
+OUT_WINDOW = 2 * W
+
+
+def tile_picked_pqmixminmodkdif_none_p_kernel(
+    tc, x_words, x_scales, d_words, d_scales, gn, w1, w2, offs, k1, n1, n2, two, n3, n4, out
+):
+    nc = tc.nc
+    with ExitStack() as ctx:
+        keep = ctx.enter_context(tc.tile_pool(name="keep", bufs=1))
+        psum = ctx.enter_context(tc.psum_pool(name="psum", bufs=1))
+
+        def sb(name, shape, dtype, tag=None):
+            return keep.tile(shape, dtype, name=name, tag=tag or name, align_bytes=64)
+
+        def load_list(name, dram):
+            tile = keep.tile(list(dram.shape), U16, name=name)
+            nc.sync.dma_start(tile[:], dram)
+            return tile
+
+        d_bytes = sb("d_bytes", [P, G], U8)
+        x_bytes = sb("x_bytes", [P, T], U8)
+        nc.vector.memset(d_bytes[:].bitcast(I32), 0)
+        nc.vector.memset(x_bytes[:].bitcast(I32), 0)
+        nc.scalar.dma_start(d_bytes[0:P:8, :].bitcast(I32), d_scales[0].bitcast(I32))
+        nc.scalar.dma_start(x_bytes[0:P:8, :].bitcast(I32), x_scales[0].bitcast(I32))
+
+        gain_rows = sb("gain_rows", [P, P], F32)
+        identity = sb("identity", [P, P], F32)
+        nc.gpsimd.memset(gain_rows[:], 0.0)
+        nc.gpsimd.dma_start(gain_rows[0:PACK, :], gn.rearrange("(b t q) one -> t b (q one)", t=PACK, q=8))
+        make_identity(nc, identity[:])
+        gain_ps = psum.tile([P, P], F32, name="bank7")
+        nc.tensor.transpose(gain_ps[:], gain_rows[:], identity[:])
+        gain = sb("gain", [P, PACK], F32)
+        nc.scalar.activation(gain[:], gain_ps[:, :PACK], COPY, scale=0.0625)
+
+        d_table = sb("d_table", [P, G], U32)
+        x_table = sb("x_table", [P, T], U32)
+        k1_t = load_list("k1_t", k1)
+        offs_t = load_list("offs_t", offs)
+        nc.sync.dma_start(d_table[:].bitcast(I32), d_words[0].rearrange("p n t -> p (n t)").bitcast(I32))
+        two_t = load_list("two_t", two)
+        n1_t = load_list("n1_t", n1)
+        n2_t = load_list("n2_t", n2)
+        nc.sync.dma_start(x_table[:].bitcast(I32), x_words[0].rearrange("p n t -> p (n t)").bitcast(I32))
+        n3_t = load_list("n3_t", n3)
+        n4_t = load_list("n4_t", n4)
+        o_win = [sb("o_win%d" % t, [P, OUT_WINDOW], F32) for t in range(PACK)]
+        h_win = [sb("h_win%d" % t, [P, S], F32) for t in range(PACK)]
+        for t in range(PACK):
+            nc.gpsimd.memset(o_win[t][:, S:], 0.0)
+
+        dk_bytes = sb("dk_bytes", [P, H], U8)
+        xq_bytes = sb("xq_bytes", [P, S], U8)
+        nc.vector.tensor_copy(dk_bytes[:], d_bytes[:].indirect(k1_t[:]))
+        nc.vector.tensor_copy(xq_bytes[:], x_bytes[:].indirect(offs_t[:]))
+        first_scales = sb("first_scales", [P, H + S], U8)
+        nc.vector.tensor_copy(
+            first_scales[:, :H].bitcast(I32).rearrange("p (t b w) -> p t b w", t=PACK, w=2),
+            dk_bytes[:].bitcast(I32).rearrange("p (b t w) -> p t b w", t=PACK, w=2),
+        )
+        nc.vector.tensor_copy(first_scales[:, H:].bitcast(I32), xq_bytes[:].bitcast(I32))
+        for r in range(1, 4):
+            nc.scalar.dma_start(first_scales[r:P:32, :].bitcast(I32), first_scales[8 * r : P : 32, :].bitcast(I32))
+
+        w2_raw = sb("w2_raw", [P, PACK, N], F32, tag="xq_bytes")
+        nc.sync.dma_start(w2_raw[:], w2.rearrange("(p t) m -> p t m", t=PACK))
+
+        dk_words = sb("dk_words", [P, H], U32)
+        dk_dealt = sb("dk_dealt", [P, H], U32)
+        xq_words = sb("xq_words", [P, S], U32)
+        nc.vector.tensor_copy(dk_words[:], d_table[:].indirect(k1_t[:]))
+        nc.vector.tensor_copy(xq_words[:], x_table[:].indirect(offs_t[:]))
+        nc.vector.tensor_copy(
+            dk_dealt[:].rearrange("p (t b q) -> p t b q", t=PACK, q=8),
+            dk_words[:].rearrange("p (b t q) -> p t b q", t=PACK, q=8),
+        )
+
+        w1_raw = sb("w1_raw", [P, PACK, N], F32, tag="d_table")
+        w1_rows = w1.rearrange("(b t q) m -> t b q m", t=PACK, q=8)
+        for t in range(PACK):
+            nc.sync.dma_start(w1_raw[:, t, :], w1_rows[t])
+
+        h_acc = [psum.tile([P, S], F32, name="bank%d" % t) for t in range(PACK)]
+        o_acc = [psum.tile([P, S], F32, name="bank%d" % (PACK + t)) for t in range(PACK)]
+        for t in range(PACK):
+            cols = slice(t * P, (t + 1) * P)
+            nc.tensor.matmul_mx(
+                out=h_acc[t][:], lhsT=dk_dealt[:, cols].bitcast(FP8X4), lhsT_scale=first_scales[:, cols],
+                rhs=xq_words[:].bitcast(FP8X4), rhs_scale=first_scales[:, H:], start=True, stop=True,
+            )
+
+        x2_bytes = sb("x2_bytes", [P, S], U8, tag="dk_words")
+        x2_scales = sb("x2_scales", [P, S], U8)
+        x2_words = sb("x2_words", [P, S], U32)
+        nc.vector.tensor_copy(x2_bytes[:], x_bytes[:].indirect(two_t[:]))
+        nc.vector.tensor_copy(x2_words[:], x_table[:].indirect(two_t[:]))
+        nc.vector.tensor_copy(x2_scales[:].bitcast(I32), x2_bytes[:].bitcast(I32))
+        for r in range(1, 4):
+            nc.sync.dma_start(x2_scales[r:P:32, :].bitcast(I32), x2_scales[8 * r : P : 32, :].bitcast(I32))
+
+        def grouped_views(grouped, raw):
+            return (
+                grouped.rearrange("p (c i t) -> p c t i", i=4, t=PACK),
+                raw.rearrange("p t (c i) -> p c t i", i=4),
+            )
+
+        w2_grouped = sb("w2_grouped", [P, PACK * N], BF16)
+        nc.vector.tensor_copy(*grouped_views(w2_grouped[:], w2_raw[:]))
+        w2_codes = sb("w2_codes", [P, N], U32)
+        w2_scales = sb("w2_scales", [P, N], U8)
+        nc.vector.quantize_mx(out=w2_codes[:].bitcast(FP8X4), scales=w2_scales[:], in_=w2_grouped[:])
+        for m in range(PACK):
+            cols = slice(m * P, (m + 1) * P)
+            nc.tensor.matmul_mx(
+                out=o_acc[m][:], lhsT=w2_codes[:, cols].bitcast(FP8X4), lhsT_scale=w2_scales[:, cols],
+                rhs=x2_words[:].bitcast(FP8X4), rhs_scale=x2_scales[:], start=True, stop=False,
+            )
+
+        g1 = [sb("g1_%d" % t, [P, S], F32) for t in range(PACK)]
+        g2 = [sb("g2_%d" % t, [P, S], F32) for t in range(PACK)]
+        pa = [sb("pa%d" % t, [P, S], F32) for t in range(PACK)]
+        pb = [sb("pb%d" % u, [P, 2, S], F32) for u in range(2)]
+        upper = [sb("upper%d" % u, [P, 2, S], F32) for u in range(2)]
+        z_pairs = [sb("z_pairs%d" % c, [P, 2, 2 * HALF], BF16) for c in range(2)]
+        z_grouped = [sb("z_grouped%d" % c, [P, PACK * HALF], BF16) for c in range(2)]
+        z_codes = [sb("z_codes%d" % c, [P, HALF], U32) for c in range(2)]
+        z_scales = [sb("z_scales%d" % c, [P, HALF], U8) for c in range(2)]
+        halves = [slice(c * HALF, (c + 1) * HALF) for c in range(2)]
+        list_halves = [slice(c * HALF // 16, (c + 1) * HALF // 16) for c in range(2)]
+
+        def differences(t, cols):
+            u, e = divmod(t, 2)
+            nc.vector.tensor_tensor(pa[t][:, cols], h_win[t][:, cols], g1[t][:, cols], ALU.subtract)
+            nc.vector.tensor_tensor(pb[u][:, e, cols], g2[t][:, cols], h_win[t][:, cols], ALU.subtract)
+
+        def clip_above(t, cols):
+            u, e = divmod(t, 2)
+            nc.vector.scalar_tensor_tensor(upper[u][:, e, cols], pb[u][:, e, cols], 0.0, pa[t][:, cols], ALU.max, ALU.min)
+
+        def clip_below(u, c):
+            nc.vector.scalar_tensor_tensor(
+                z_pairs[c][:, u, :].rearrange("p (j e) -> p j e", e=2),
+                pb[u][:, :, halves[c]].rearrange("p e j -> p j e"), 0.0,
+                upper[u][:, :, halves[c]].rearrange("p e j -> p j e"), ALU.min, ALU.max,
+            )
+
+        def weave(c):
+            nc.vector.tensor_copy(
+                z_grouped[c][:].bitcast(F32).rearrange("p (j u) -> p j u", u=2),
+                z_pairs[c][:].bitcast(F32).rearrange("p u j -> p j u"),
+            )
+
+        def leave_h(t):
+            nc.scalar.activation(h_win[t][:], h_acc[t][:], COPY, scale=gain[:, t : t + 1])
+
+        leave_h(0)
+        for t in range(PACK):
+            for c in range(2):
+                nc.scalar.activation(g1[t][:, halves[c]], h_win[t][:].indirect(n1_t[:, list_halves[c]]), COPY)
+                if c == 1 and t + 1 < PACK:
+                    leave_h(t + 1)
+                nc.scalar.activation(g2[t][:, halves[c]], h_win[t][:].indirect(n2_t[:, list_halves[c]]), COPY)
+            if t < PACK - 1:
+                differences(t, slice(0, S))
+                clip_above(t, slice(0, S))
+            if t == 1:
+                clip_below(0, 0)
+                clip_below(0, 1)
+        last = PACK - 1
+        w1_grouped = [sb("w1_grouped%d" % c, [P, PACK * HALF], BF16, tag="h_win%d" % c) for c in range(2)]
+        w1_codes = [sb("w1_codes%d" % c, [P, HALF], U32) for c in range(2)]
+        w1_scales = [sb("w1_scales%d" % c, [P, HALF], U8) for c in range(2)]
+        for c in range(2):
+            nc.scalar.copy(*grouped_views(w1_grouped[c][:], w1_raw[:, :, halves[c]]))
+        differences(last, halves[0])
+        clip_above(last, halves[0])
+        differences(last, halves[1])
+        clip_below(1, 0)
+        clip_above(last, halves[1])
+        weave(0)
+        clip_below(1, 1)
+        nc.vector.quantize_mx(out=w1_codes[0][:].bitcast(FP8X4), scales=w1_scales[0][:], in_=w1_grouped[0][:])
+        nc.vector.quantize_mx(out=z_codes[0][:].bitcast(FP8X4), scales=z_scales[0][:], in_=z_grouped[0][:])
+        weave(1)
+        nc.vector.quantize_mx(out=z_codes[1][:].bitcast(FP8X4), scales=z_scales[1][:], in_=z_grouped[1][:])
+        nc.vector.quantize_mx(out=w1_codes[1][:].bitcast(FP8X4), scales=w1_scales[1][:], in_=w1_grouped[1][:])
+
+        for side in range(2):
+            for c in range(2):
+                for k in range(2):
+                    m, cols = 2 * side + k, slice(k * P, (k + 1) * P)
+                    nc.tensor.matmul_mx(
+                        out=o_acc[m][:, halves[c]], lhsT=w1_codes[side][:, cols].bitcast(FP8X4),
+                        lhsT_scale=w1_scales[side][:, cols],
+                        rhs=z_codes[c][:].bitcast(FP8X4), rhs_scale=z_scales[c][:], start=False, stop=(c == 1),
+                    )
+
+        old = [sb("old%d" % m, [P, W], F32) for m in range(PACK)]
+        pull = [sb("pull%d" % m, [P, W], F32) for m in range(PACK)]
+
+        def fetch_pull(m):
+            nc.scalar.activation(pull[m][:], o_win[m][:].indirect(n4_t[:]), COPY, scale=-0.5)
+
+        def fetch_old(m):
+            nc.scalar.activation(old[m][:], o_win[m][:].indirect(n3_t[:]), COPY)
+
+        def put(m):
+            nc.vector.tensor_tensor(o_win[m][:].indirect(n3_t[:]), old[m][:], pull[m][:], ALU.add)
+            nc.sync.dma_start(out[m * P : (m + 1) * P, :], o_win[m][:, :S])
+
+        nc.vector.tensor_copy(o_win[0][:, :S], o_acc[0][:])
+        nc.scalar.copy(o_win[1][:, :S], o_acc[1][:])
+        fetch_pull(0)
+        nc.vector.tensor_copy(old[0][:], o_win[0][:].indirect(n3_t[:]))
+        put(0)
+        nc.scalar.copy(o_win[3][:, :S], o_acc[3][:])
+        fetch_pull(1)
+        fetch_pull(3)
+        nc.vector.tensor_tensor(old[3][:], o_win[3][:].indirect(n3_t[:]), pull[3][:], ALU.add)
+        nc.scalar.copy(o_win[2][:, :S], o_acc[2][:])
+        fetch_old(1)
+        put(1)
+        fetch_pull(2)
+        fetch_old(2)
+        put(2)
+        nc.scalar.activation(o_win[3][:].indirect(n3_t[:]), old[3][:], COPY)
+        nc.scalar.dma_start(out[3 * P :, :], o_win[3][:, :S])

@@ -40,10 +40,6 @@ def tile_picked_pqmixminmodkdif_none_p_kernel(
 
         d_bytes = sb("d_bytes", [P, G], U8)
         x_bytes = sb("x_bytes", [P, T], U8)
-        nc.vector.memset(d_bytes[:].bitcast(I32), 0)
-        nc.vector.memset(x_bytes[:].bitcast(I32), 0)
-        nc.scalar.dma_start(d_bytes[0:P:8, :].bitcast(I32), d_scales[0].bitcast(I32))
-        nc.scalar.dma_start(x_bytes[0:P:8, :].bitcast(I32), x_scales[0].bitcast(I32))
 
         gain_rows = sb("gain_rows", [P, P], F32)
         identity = sb("identity", [P, P], F32)
@@ -57,13 +53,19 @@ def tile_picked_pqmixminmodkdif_none_p_kernel(
 
         d_table = sb("d_table", [P, G], U32)
         x_table = sb("x_table", [P, T], U32)
-        k1_t = load_list("k1_t", k1)
         offs_t = load_list("offs_t", offs)
-        nc.sync.dma_start(d_table[:].bitcast(I32), d_words[0].rearrange("p n t -> p (n t)").bitcast(I32))
+        nc.sync.dma_start(x_bytes[:].bitcast(I32), x_scales[0].bitcast(I32).unsqueeze(1).to_broadcast([16, 8, T // 4]))
         two_t = load_list("two_t", two)
+        k1_t = load_list("k1_t", k1)
+        nc.sync.dma_start(d_bytes[:].bitcast(I32), d_scales[0].bitcast(I32).unsqueeze(1).to_broadcast([16, 8, G // 4]))
         n1_t = load_list("n1_t", n1)
         n2_t = load_list("n2_t", n2)
+        w2_rows = w2.rearrange("(p t) m -> p t m", t=PACK)
+        w2_raw = [sb("w2_raw%d" % c, [P, PACK, HALF], F32) for c in range(2)]
+        nc.sync.dma_start(w2_raw[0][:], w2_rows[:, :, :HALF])
         nc.sync.dma_start(x_table[:].bitcast(I32), x_words[0].rearrange("p n t -> p (n t)").bitcast(I32))
+        nc.sync.dma_start(d_table[:].bitcast(I32), d_words[0].rearrange("p n t -> p (n t)").bitcast(I32))
+        nc.sync.dma_start(w2_raw[1][:], w2_rows[:, :, HALF:])
         n3_t = load_list("n3_t", n3)
         n4_t = load_list("n4_t", n4)
         o_win = [sb("o_win%d" % t, [P, OUT_WINDOW], F32) for t in range(PACK)]
@@ -71,36 +73,35 @@ def tile_picked_pqmixminmodkdif_none_p_kernel(
         for t in range(PACK):
             nc.gpsimd.memset(o_win[t][:, S:], 0.0)
 
+        def settle_scale_rows(plane, queues):
+            for q in range(4):
+                queues[q % len(queues)].dma_start(
+                    plane[32 * q : 32 * q + 4, :].bitcast(I32), plane[32 * q + 4 : 32 * q + 32 : 8, :].bitcast(I32)
+                )
+
         dk_bytes = sb("dk_bytes", [P, H], U8)
-        xq_bytes = sb("xq_bytes", [P, S], U8)
+        x_picked_bytes = sb("x_picked_bytes", [P, 2 * S], U8)
+        nc.vector.tensor_copy(x_picked_bytes[:, :S], x_bytes[:].indirect(offs_t[:]))
+        nc.vector.tensor_copy(x_picked_bytes[:, S:], x_bytes[:].indirect(two_t[:]))
         nc.vector.tensor_copy(dk_bytes[:], d_bytes[:].indirect(k1_t[:]))
-        nc.vector.tensor_copy(xq_bytes[:], x_bytes[:].indirect(offs_t[:]))
-        first_scales = sb("first_scales", [P, H + S], U8)
+        first_scales = sb("first_scales", [P, H + 2 * S], U8)
+        nc.vector.tensor_copy(first_scales[:, H:].bitcast(I32), x_picked_bytes[:].bitcast(I32))
         nc.vector.tensor_copy(
             first_scales[:, :H].bitcast(I32).rearrange("p (t b w) -> p t b w", t=PACK, w=2),
             dk_bytes[:].bitcast(I32).rearrange("p (b t w) -> p t b w", t=PACK, w=2),
         )
-        nc.vector.tensor_copy(first_scales[:, H:].bitcast(I32), xq_bytes[:].bitcast(I32))
-        for r in range(1, 4):
-            nc.scalar.dma_start(first_scales[r:P:32, :].bitcast(I32), first_scales[8 * r : P : 32, :].bitcast(I32))
-
-        w2_raw = sb("w2_raw", [P, PACK, N], F32, tag="xq_bytes")
-        nc.sync.dma_start(w2_raw[:], w2.rearrange("(p t) m -> p t m", t=PACK))
+        settle_scale_rows(first_scales, (nc.sync,))
 
         dk_words = sb("dk_words", [P, H], U32)
         dk_dealt = sb("dk_dealt", [P, H], U32)
         xq_words = sb("xq_words", [P, S], U32)
-        nc.vector.tensor_copy(dk_words[:], d_table[:].indirect(k1_t[:]))
         nc.vector.tensor_copy(xq_words[:], x_table[:].indirect(offs_t[:]))
+        nc.vector.tensor_copy(dk_words[:], d_table[:].indirect(k1_t[:]))
         nc.vector.tensor_copy(
             dk_dealt[:].rearrange("p (t b q) -> p t b q", t=PACK, q=8),
             dk_words[:].rearrange("p (b t q) -> p t b q", t=PACK, q=8),
         )
 
-        w1_raw = sb("w1_raw", [P, PACK, N], F32, tag="d_table")
-        w1_rows = w1.rearrange("(b t q) m -> t b q m", t=PACK, q=8)
-        for t in range(PACK):
-            nc.sync.dma_start(w1_raw[:, t, :], w1_rows[t])
 
         h_acc = [psum.tile([P, S], F32, name="bank%d" % t) for t in range(PACK)]
         o_acc = [psum.tile([P, S], F32, name="bank%d" % (PACK + t)) for t in range(PACK)]
@@ -108,17 +109,16 @@ def tile_picked_pqmixminmodkdif_none_p_kernel(
             cols = slice(t * P, (t + 1) * P)
             nc.tensor.matmul_mx(
                 out=h_acc[t][:], lhsT=dk_dealt[:, cols].bitcast(FP8X4), lhsT_scale=first_scales[:, cols],
-                rhs=xq_words[:].bitcast(FP8X4), rhs_scale=first_scales[:, H:], start=True, stop=True,
+                rhs=xq_words[:].bitcast(FP8X4), rhs_scale=first_scales[:, H : H + S], start=True, stop=True,
             )
 
-        x2_bytes = sb("x2_bytes", [P, S], U8, tag="dk_words")
-        x2_scales = sb("x2_scales", [P, S], U8)
-        x2_words = sb("x2_words", [P, S], U32)
-        nc.vector.tensor_copy(x2_bytes[:], x_bytes[:].indirect(two_t[:]))
+        x2_words = sb("x2_words", [P, S], U32, tag="dk_words")
         nc.vector.tensor_copy(x2_words[:], x_table[:].indirect(two_t[:]))
-        nc.vector.tensor_copy(x2_scales[:].bitcast(I32), x2_bytes[:].bitcast(I32))
-        for r in range(1, 4):
-            nc.sync.dma_start(x2_scales[r:P:32, :].bitcast(I32), x2_scales[8 * r : P : 32, :].bitcast(I32))
+
+        w1_raw = sb("w1_raw", [P, PACK, N], F32, tag="d_table")
+        w1_rows = w1.rearrange("(b t q) m -> t b q m", t=PACK, q=8)
+        for t in range(PACK):
+            nc.sync.dma_start(w1_raw[:, t, :], w1_rows[t])
 
         def grouped_views(grouped, raw):
             return (
@@ -127,15 +127,16 @@ def tile_picked_pqmixminmodkdif_none_p_kernel(
             )
 
         w2_grouped = sb("w2_grouped", [P, PACK * N], BF16)
-        nc.vector.tensor_copy(*grouped_views(w2_grouped[:], w2_raw[:]))
+        for c in range(2):
+            nc.scalar.copy(*grouped_views(w2_grouped[:, c * PACK * HALF : (c + 1) * PACK * HALF], w2_raw[c][:]))
         w2_codes = sb("w2_codes", [P, N], U32)
-        w2_scales = sb("w2_scales", [P, N], U8)
+        w2_scales = sb("w2_scales", [P, N], U8, tag="dk_dealt")
         nc.vector.quantize_mx(out=w2_codes[:].bitcast(FP8X4), scales=w2_scales[:], in_=w2_grouped[:])
         for m in range(PACK):
             cols = slice(m * P, (m + 1) * P)
             nc.tensor.matmul_mx(
                 out=o_acc[m][:], lhsT=w2_codes[:, cols].bitcast(FP8X4), lhsT_scale=w2_scales[:, cols],
-                rhs=x2_words[:].bitcast(FP8X4), rhs_scale=x2_scales[:], start=True, stop=False,
+                rhs=x2_words[:].bitcast(FP8X4), rhs_scale=first_scales[:, H + S :], start=True, stop=False,
             )
 
         g1 = [sb("g1_%d" % t, [P, S], F32) for t in range(PACK)]
@@ -150,9 +151,11 @@ def tile_picked_pqmixminmodkdif_none_p_kernel(
         halves = [slice(c * HALF, (c + 1) * HALF) for c in range(2)]
         list_halves = [slice(c * HALF // 16, (c + 1) * HALF // 16) for c in range(2)]
 
-        def differences(t, cols):
+        def form_pa(t):
+            nc.vector.tensor_tensor(pa[t][:], h_win[t][:], g1[t][:], ALU.subtract)
+
+        def form_pb(t, cols):
             u, e = divmod(t, 2)
-            nc.vector.tensor_tensor(pa[t][:, cols], h_win[t][:, cols], g1[t][:, cols], ALU.subtract)
             nc.vector.tensor_tensor(pb[u][:, e, cols], g2[t][:, cols], h_win[t][:, cols], ALU.subtract)
 
         def clip_above(t, cols):
@@ -166,8 +169,8 @@ def tile_picked_pqmixminmodkdif_none_p_kernel(
                 upper[u][:, :, halves[c]].rearrange("p e j -> p j e"), ALU.min, ALU.max,
             )
 
-        def weave(c):
-            nc.vector.tensor_copy(
+        def weave(c, copy):
+            copy(
                 z_grouped[c][:].bitcast(F32).rearrange("p (j u) -> p j u", u=2),
                 z_pairs[c][:].bitcast(F32).rearrange("p u j -> p j u"),
             )
@@ -179,11 +182,16 @@ def tile_picked_pqmixminmodkdif_none_p_kernel(
         for t in range(PACK):
             for c in range(2):
                 nc.scalar.activation(g1[t][:, halves[c]], h_win[t][:].indirect(n1_t[:, list_halves[c]]), COPY)
-                if c == 1 and t + 1 < PACK:
-                    leave_h(t + 1)
-                nc.scalar.activation(g2[t][:, halves[c]], h_win[t][:].indirect(n2_t[:, list_halves[c]]), COPY)
+            if t + 1 < PACK:
+                leave_h(t + 1)
+            for c in range(2):
+                if t == 0:
+                    nc.vector.tensor_copy(g2[t][:, halves[c]], h_win[t][:].indirect(n2_t[:, list_halves[c]]))
+                else:
+                    nc.scalar.activation(g2[t][:, halves[c]], h_win[t][:].indirect(n2_t[:, list_halves[c]]), COPY)
+            form_pa(t)
             if t < PACK - 1:
-                differences(t, slice(0, S))
+                form_pb(t, slice(0, S))
                 clip_above(t, slice(0, S))
             if t == 1:
                 clip_below(0, 0)
@@ -194,16 +202,16 @@ def tile_picked_pqmixminmodkdif_none_p_kernel(
         w1_scales = [sb("w1_scales%d" % c, [P, HALF], U8) for c in range(2)]
         for c in range(2):
             nc.scalar.copy(*grouped_views(w1_grouped[c][:], w1_raw[:, :, halves[c]]))
-        differences(last, halves[0])
+        form_pb(last, halves[0])
         clip_above(last, halves[0])
-        differences(last, halves[1])
+        form_pb(last, halves[1])
         clip_below(1, 0)
         clip_above(last, halves[1])
-        weave(0)
+        weave(0, nc.vector.tensor_copy)
         clip_below(1, 1)
         nc.vector.quantize_mx(out=w1_codes[0][:].bitcast(FP8X4), scales=w1_scales[0][:], in_=w1_grouped[0][:])
         nc.vector.quantize_mx(out=z_codes[0][:].bitcast(FP8X4), scales=z_scales[0][:], in_=z_grouped[0][:])
-        weave(1)
+        weave(1, nc.vector.tensor_copy)
         nc.vector.quantize_mx(out=z_codes[1][:].bitcast(FP8X4), scales=z_scales[1][:], in_=z_grouped[1][:])
         nc.vector.quantize_mx(out=w1_codes[1][:].bitcast(FP8X4), scales=w1_scales[1][:], in_=w1_grouped[1][:])
 

@@ -130,7 +130,7 @@ def tile_picked_pqmixminmodkdif_none_p_kernel(
         for c in range(2):
             nc.scalar.copy(*grouped_views(w2_grouped[:, c * PACK * HALF : (c + 1) * PACK * HALF], w2_raw[c][:]))
         w2_codes = sb("w2_codes", [P, N], U32)
-        w2_scales = sb("w2_scales", [P, N], U8, tag="dk_dealt")
+        w2_scales = sb("w2_scales", [P, N], U8, tag="x_table")
         nc.vector.quantize_mx(out=w2_codes[:].bitcast(FP8X4), scales=w2_scales[:], in_=w2_grouped[:])
         for m in range(PACK):
             cols = slice(m * P, (m + 1) * P)
@@ -185,7 +185,7 @@ def tile_picked_pqmixminmodkdif_none_p_kernel(
             if t + 1 < PACK:
                 leave_h(t + 1)
             for c in range(2):
-                if t == 0:
+                if 2 * t + c < 3:
                     nc.vector.tensor_copy(g2[t][:, halves[c]], h_win[t][:].indirect(n2_t[:, list_halves[c]]))
                 else:
                     nc.scalar.activation(g2[t][:, halves[c]], h_win[t][:].indirect(n2_t[:, list_halves[c]]), COPY)
@@ -207,7 +207,7 @@ def tile_picked_pqmixminmodkdif_none_p_kernel(
         form_pb(last, halves[1])
         clip_below(1, 0)
         clip_above(last, halves[1])
-        weave(0, nc.vector.tensor_copy)
+        weave(0, nc.scalar.copy)
         clip_below(1, 1)
         nc.vector.quantize_mx(out=w1_codes[0][:].bitcast(FP8X4), scales=w1_scales[0][:], in_=w1_grouped[0][:])
         nc.vector.quantize_mx(out=z_codes[0][:].bitcast(FP8X4), scales=z_scales[0][:], in_=z_grouped[0][:])

from contextlib import ExitStack

import concourse.mybir as mybir
from concourse.masks import make_identity

K, T, S, N, G, H, W = 512, 1024, 512, 512, 2048, 512, 384
FLOPS = 3 * 2 * 512 * 512 * 512

F32 = mybir.dt.float32
BF16 = mybir.dt.bfloat16
U32 = mybir.dt.uint32
I32 = mybir.dt.int32
U16 = mybir.dt.uint16
U8 = mybir.dt.uint8
FP8X4 = mybir.dt.float8_e4m3fn_x4
ALU = mybir.AluOpType
COPY = mybir.ActivationFunctionType.Copy

P = 128
PACK = 4
HALF = S // 2
OUT_WINDOW = 2 * W


def tile_picked_pqmixminmodkdif_none_p_kernel(
    tc, x_words, x_scales, d_words, d_scales, gn, w1, w2, offs, k1, n1, n2, two, n3, n4, out
):
    nc = tc.nc
    with ExitStack() as ctx:
        keep = ctx.enter_context(tc.tile_pool(name="keep", bufs=1))
        psum = ctx.enter_context(tc.psum_pool(name="psum", bufs=1))

        def sb(name, shape, dtype, tag=None):
            return keep.tile(shape, dtype, name=name, tag=tag or name, align_bytes=64)

        def load_list(name, dram):
            tile = keep.tile(list(dram.shape), U16, name=name)
            nc.sync.dma_start(tile[:], dram)
            return tile

        d_bytes = sb("d_bytes", [P, G], U8)
        x_bytes = sb("x_bytes", [P, T], U8)

        gain_rows = sb("gain_rows", [P, P], F32)
        identity = sb("identity", [P, P], F32)
        nc.gpsimd.memset(gain_rows[:], 0.0)
        nc.gpsimd.dma_start(gain_rows[0:PACK, :], gn.rearrange("(b t q) one -> t b (q one)", t=PACK, q=8))
        make_identity(nc, identity[:])
        gain_ps = psum.tile([P, P], F32, name="bank7")
        nc.tensor.transpose(gain_ps[:], gain_rows[:], identity[:])
        gain = sb("gain", [P, PACK], F32)
        nc.scalar.activation(gain[:], gain_ps[:, :PACK], COPY, scale=0.0625)

        d_table = sb("d_table", [P, G], U32)
        x_table = sb("x_table", [P, T], U32)
        offs_t = load_list("offs_t", offs)
        nc.sync.dma_start(x_bytes[:].bitcast(I32), x_scales[0].bitcast(I32).unsqueeze(1).to_broadcast([16, 8, T // 4]))
        two_t = load_list("two_t", two)
        k1_t = load_list("k1_t", k1)
        nc.sync.dma_start(d_bytes[:].bitcast(I32), d_scales[0].bitcast(I32).unsqueeze(1).to_broadcast([16, 8, G // 4]))
        n1_t = load_list("n1_t", n1)
        n2_t = load_list("n2_t", n2)
        w2_rows = w2.rearrange("(p t) m -> p t m", t=PACK)
        w2_raw = [sb("w2_raw%d" % c, [P, PACK, HALF], F32) for c in range(2)]
        nc.sync.dma_start(w2_raw[0][:], w2_rows[:, :, :HALF])
        nc.sync.dma_start(x_table[:].bitcast(I32), x_words[0].rearrange("p n t -> p (n t)").bitcast(I32))
        nc.sync.dma_start(d_table[:].bitcast(I32), d_words[0].rearrange("p n t -> p (n t)").bitcast(I32))
        nc.sync.dma_start(w2_raw[1][:], w2_rows[:, :, HALF:])
        n3_t = load_list("n3_t", n3)
        n4_t = load_list("n4_t", n4)
        o_win = [sb("o_win%d" % t, [P, OUT_WINDOW], F32) for t in range(PACK)]
        h_win = [sb("h_win%d" % t, [P, S], F32) for t in range(PACK)]
        for t in range(PACK):
            nc.gpsimd.memset(o_win[t][:, S:], 0.0)

        def settle_scale_rows(plane, queues):
            for q in range(4):
                queues[q % len(queues)].dma_start(
                    plane[32 * q : 32 * q + 4, :].bitcast(I32), plane[32 * q + 4 : 32 * q + 32 : 8, :].bitcast(I32)
                )

        dk_bytes = sb("dk_bytes", [P, H], U8)
        x_picked_bytes = sb("x_picked_bytes", [P, 2 * S], U8)
        nc.vector.tensor_copy(x_picked_bytes[:, :S], x_bytes[:].indirect(offs_t[:]))
        nc.vector.tensor_copy(x_picked_bytes[:, S:], x_bytes[:].indirect(two_t[:]))
        nc.vector.tensor_copy(dk_bytes[:], d_bytes[:].indirect(k1_t[:]))
        first_scales = sb("first_scales", [P, H + 2 * S], U8)
        nc.vector.tensor_copy(first_scales[:, H:].bitcast(I32), x_picked_bytes[:].bitcast(I32))
        nc.vector.tensor_copy(
            first_scales[:, :H].bitcast(I32).rearrange("p (t b w) -> p t b w", t=PACK, w=2),
            dk_bytes[:].bitcast(I32).rearrange("p (b t w) -> p t b w", t=PACK, w=2),
        )
        settle_scale_rows(first_scales, (nc.sync,))

        dk_words = sb("dk_words", [P, H], U32)
        dk_dealt = sb("dk_dealt", [P, H], U32)
        xq_words = sb("xq_words", [P, S], U32)
        nc.vector.tensor_copy(xq_words[:], x_table[:].indirect(offs_t[:]))
        nc.vector.tensor_copy(dk_words[:], d_table[:].indirect(k1_t[:]))
        nc.vector.tensor_copy(
            dk_dealt[:].rearrange("p (t b q) -> p t b q", t=PACK, q=8),
            dk_words[:].rearrange("p (b t q) -> p t b q", t=PACK, q=8),
        )


        h_acc = [psum.tile([P, S], F32, name="bank%d" % t) for t in range(PACK)]
        o_acc = [psum.tile([P, S], F32, name="bank%d" % (PACK + t)) for t in range(PACK)]
        for t in range(PACK):
            cols = slice(t * P, (t + 1) * P)
            nc.tensor.matmul_mx(
                out=h_acc[t][:], lhsT=dk_dealt[:, cols].bitcast(FP8X4), lhsT_scale=first_scales[:, cols],
                rhs=xq_words[:].bitcast(FP8X4), rhs_scale=first_scales[:, H : H + S], start=True, stop=True,
            )

        x2_words = sb("x2_words", [P, S], U32, tag="dk_words")
        nc.vector.tensor_copy(x2_words[:], x_table[:].indirect(two_t[:]))

        w1_raw = sb("w1_raw", [P, PACK, N], F32, tag="d_table")
        w1_rows = w1.rearrange("(b t q) m -> t b q m", t=PACK, q=8)
        for t in range(PACK):
            nc.sync.dma_start(w1_raw[:, t, :], w1_rows[t])

        def grouped_views(grouped, raw):
            return (
                grouped.rearrange("p (c i t) -> p c t i", i=4, t=PACK),
                raw.rearrange("p t (c i) -> p c t i", i=4),
            )

        w2_grouped = sb("w2_grouped", [P, PACK * N], BF16)
        for c in range(2):
            nc.scalar.copy(*grouped_views(w2_grouped[:, c * PACK * HALF : (c + 1) * PACK * HALF], w2_raw[c][:]))
        w2_codes = sb("w2_codes", [P, N], U32)
        w2_scales = sb("w2_scales", [P, N], U8, tag="x_table")
        nc.vector.quantize_mx(out=w2_codes[:].bitcast(FP8X4), scales=w2_scales[:], in_=w2_grouped[:])
        for m in range(PACK):
            cols = slice(m * P, (m + 1) * P)
            nc.tensor.matmul_mx(
                out=o_acc[m][:], lhsT=w2_codes[:, cols].bitcast(FP8X4), lhsT_scale=w2_scales[:, cols],
                rhs=x2_words[:].bitcast(FP8X4), rhs_scale=first_scales[:, H + S :], start=True, stop=False,
            )

        g1 = [sb("g1_%d" % t, [P, S], F32) for t in range(PACK)]
        g2 = [sb("g2_%d" % t, [P, S], F32) for t in range(PACK)]
        pa = [sb("pa%d" % t, [P, S], F32) for t in range(PACK)]
        pb = [sb("pb%d" % u, [P, 2, S], F32) for u in range(2)]
        upper = [sb("upper%d" % u, [P, 2, S], F32) for u in range(2)]
        z_pairs = [sb("z_pairs%d" % c, [P, 2, 2 * HALF], BF16) for c in range(2)]
        z_grouped = [sb("z_grouped%d" % c, [P, PACK * HALF], BF16) for c in range(2)]
        z_codes = [sb("z_codes%d" % c, [P, HALF], U32) for c in range(2)]
        z_scales = [sb("z_scales%d" % c, [P, HALF], U8) for c in range(2)]
        halves = [slice(c * HALF, (c + 1) * HALF) for c in range(2)]
        list_halves = [slice(c * HALF // 16, (c + 1) * HALF // 16) for c in range(2)]

        def form_pa(t):
            nc.vector.tensor_tensor(pa[t][:], h_win[t][:], g1[t][:], ALU.subtract)

        def form_pb(t, cols):
            u, e = divmod(t, 2)
            nc.vector.tensor_tensor(pb[u][:, e, cols], g2[t][:, cols], h_win[t][:, cols], ALU.subtract)

        def clip_above(t, cols):
            u, e = divmod(t, 2)
            nc.vector.scalar_tensor_tensor(upper[u][:, e, cols], pb[u][:, e, cols], 0.0, pa[t][:, cols], ALU.max, ALU.min)

        def clip_below(u, c):
            nc.vector.scalar_tensor_tensor(
                z_pairs[c][:, u, :].rearrange("p (j e) -> p j e", e=2),
                pb[u][:, :, halves[c]].rearrange("p e j -> p j e"), 0.0,
                upper[u][:, :, halves[c]].rearrange("p e j -> p j e"), ALU.min, ALU.max,
            )

        def weave(c, copy):
            copy(
                z_grouped[c][:].bitcast(F32).rearrange("p (j u) -> p j u", u=2),
                z_pairs[c][:].bitcast(F32).rearrange("p u j -> p j u"),
            )

        def leave_h(t):
            nc.scalar.activation(h_win[t][:], h_acc[t][:], COPY, scale=gain[:, t : t + 1])

        leave_h(0)
        for t in range(PACK):
            for c in range(2):
                nc.scalar.activation(g1[t][:, halves[c]], h_win[t][:].indirect(n1_t[:, list_halves[c]]), COPY)
            if t + 1 < PACK:
                leave_h(t + 1)
            for c in range(2):
                if 2 * t + c < 3:
                    nc.vector.tensor_copy(g2[t][:, halves[c]], h_win[t][:].indirect(n2_t[:, list_halves[c]]))
                else:
                    nc.scalar.activation(g2[t][:, halves[c]], h_win[t][:].indirect(n2_t[:, list_halves[c]]), COPY)
            form_pa(t)
            if t < PACK - 1:
                form_pb(t, slice(0, S))
                clip_above(t, slice(0, S))
            if t == 1:
                clip_below(0, 0)
                clip_below(0, 1)
        last = PACK - 1
        w1_grouped = [sb("w1_grouped%d" % c, [P, PACK * HALF], BF16, tag="h_win%d" % c) for c in range(2)]
        w1_codes = [sb("w1_codes%d" % c, [P, HALF], U32) for c in range(2)]
        w1_scales = [sb("w1_scales%d" % c, [P, HALF], U8) for c in range(2)]
        for c in range(2):
            nc.scalar.copy(*grouped_views(w1_grouped[c][:], w1_raw[:, :, halves[c]]))
        form_pb(last, halves[0])
        clip_above(last, halves[0])
        form_pb(last, halves[1])
        clip_below(1, 0)
        clip_above(last, halves[1])
        weave(0, nc.scalar.copy)
        clip_below(1, 1)
        nc.vector.quantize_mx(out=w1_codes[0][:].bitcast(FP8X4), scales=w1_scales[0][:], in_=w1_grouped[0][:])
        nc.vector.quantize_mx(out=z_codes[0][:].bitcast(FP8X4), scales=z_scales[0][:], in_=z_grouped[0][:])
        weave(1, nc.vector.tensor_copy)
        nc.vector.quantize_mx(out=z_codes[1][:].bitcast(FP8X4), scales=z_scales[1][:], in_=z_grouped[1][:])
        nc.vector.quantize_mx(out=w1_codes[1][:].bitcast(FP8X4), scales=w1_scales[1][:], in_=w1_grouped[1][:])

        for side in range(2):
            for c in range(2):
                for k in range(2):
                    m, cols = 2 * side + k, slice(k * P, (k + 1) * P)
                    nc.tensor.matmul_mx(
                        out=o_acc[m][:, halves[c]], lhsT=w1_codes[side][:, cols].bitcast(FP8X4),
                        lhsT_scale=w1_scales[side][:, cols],
                        rhs=z_codes[c][:].bitcast(FP8X4), rhs_scale=z_scales[c][:], start=False, stop=(c == 1),
                    )

        old = [sb("old%d" % m, [P, W], F32) for m in range(PACK)]
        pull = [sb("pull%d" % m, [P, W], F32) for m in range(PACK)]

        def fetch_pull(m):
            nc.scalar.activation(pull[m][:], o_win[m][:].indirect(n4_t[:]), COPY, scale=-0.5)

        def fetch_old(m):
            nc.scalar.activation(old[m][:], o_win[m][:].indirect(n3_t[:]), COPY)

        def put(m):
            nc.vector.tensor_tensor(o_win[m][:].indirect(n3_t[:]), old[m][:], pull[m][:], ALU.add)
            nc.sync.dma_start(out[m * P : (m + 1) * P, :], o_win[m][:, :S])

        nc.vector.tensor_copy(o_win[0][:, :S], o_acc[0][:])
        nc.scalar.copy(o_win[1][:, :S], o_acc[1][:])
        fetch_pull(0)
        nc.vector.tensor_copy(old[0][:], o_win[0][:].indirect(n3_t[:]))
        put(0)
        nc.scalar.copy(o_win[3][:, :S], o_acc[3][:])
        fetch_pull(1)
        fetch_pull(3)
        nc.vector.tensor_tensor(old[3][:], o_win[3][:].indirect(n3_t[:]), pull[3][:], ALU.add)
        nc.scalar.copy(o_win[2][:, :S], o_acc[2][:])
        fetch_old(1)
        put(1)
        fetch_pull(2)
        fetch_old(2)
        put(2)
        nc.scalar.activation(o_win[3][:].indirect(n3_t[:]), old[3][:], COPY)
        nc.scalar.dma_start(out[3 * P :, :], o_win[3][:, :S])
